import numpy as np
import ml_dtypes


def mxq(x, axis, fmt="e4m3"):
    dtype, down = {"e4m3": (ml_dtypes.float8_e4m3fn, 7), "e5m2": (ml_dtypes.float8_e5m2, 14)}[fmt]
    v = np.moveaxis(np.asarray(x, np.float32).astype(ml_dtypes.bfloat16).astype(np.float64), axis, -1)
    blocks = v.reshape(v.shape[:-1] + (-1, 32))
    amax = np.abs(blocks).max(-1, keepdims=True)
    byte = np.maximum(np.where(amax > 0, np.frexp(amax)[1] - 1 + 127, 0) - down, 1)
    scale = np.exp2(byte - 127.0)
    codes = (blocks / scale).astype(np.float32).astype(dtype).astype(np.float64)
    return np.moveaxis((codes * scale).reshape(v.shape), -1, axis)


WIDE = False


def mx_kscale(k):
    if not WIDE:
        return np.ones(k)
    levels = np.array([10, -10, 5, -5, 0])
    if k % 512:
        return np.exp2(np.random.permutation(np.resize(levels, k // 32))).repeat(32)
    a = np.empty((k // 512, 16))
    for p in range(k // 512):
        a[p, :8] = np.random.permutation(np.resize(levels, 8))
        for g in range(8):
            far = levels[np.abs(levels - a[p, g]) >= 10]
            a[p, g + 8] = far[np.random.randint(len(far))]
    return np.exp2(a.ravel()).repeat(32)


def f64(x):
    return np.asarray(x).astype(np.float64)


def striped(idx):
    return np.tile(idx.reshape(-1, 16).T, (8, 1)).astype(np.uint16)


def unstriped(offs):
    return offs[:16].T.reshape(-1).astype(np.int64)


def striped8(idx):
    return np.concatenate([x.reshape(-1, 16).T for x in idx]).astype(np.uint16)


def runs(offs, k):
    lists = np.stack([offs[16 * r : 16 * r + 16].T.reshape(-1) for r in range(8)]).astype(np.int64)
    return lists[np.arange(k) % 512 // 64]


def pack_weight(w):
    k, n = w.shape
    w = f64(np.asarray(w, np.float32).astype(ml_dtypes.bfloat16)).reshape(k // 32, 32, n)
    amax = np.abs(w).max(1)
    byte = np.clip(np.where(amax > 0, np.frexp(amax)[1] - 1 + 127 - 7, 1), 1, 254)
    scaled = (w * np.exp2(127.0 - byte)[:, None, :]).reshape(k, n).astype(np.float32)
    words = np.ascontiguousarray(scaled.reshape(k // 512, 128, 4, n).transpose(0, 1, 3, 2)).astype(ml_dtypes.float8_e4m3fn).view(np.uint8)
    return words, np.ascontiguousarray(byte.astype(np.uint8).reshape(k // 512, 16, n))


def unpack_weight(words, scales):
    g, p, n, _ = words.shape
    vals = np.ascontiguousarray(words).view(ml_dtypes.float8_e4m3fn).astype(np.float64) * np.repeat(np.exp2(scales.astype(np.float64) - 127.0), 8, axis=1)[..., None]
    return vals.transpose(0, 1, 3, 2).reshape(g * 512, n)

def planes(y):
    n, m = y.shape
    v = y.astype(np.float32).astype(ml_dtypes.bfloat16).astype(np.float64).reshape(n // 32, 32, m)
    top = np.abs(v).max(1)
    byte = np.clip(np.where(top > 0, np.frexp(top)[1] - 1 + 127 - 7, 1), 1, 254)
    codes = (v * np.exp2(127.0 - byte)[:, None, :]).reshape(n, m).astype(np.float32).astype(ml_dtypes.float8_e4m3fn).view(np.uint8)
    words = codes.reshape(n // 512, 128, 4, m).transpose(0, 1, 3, 2)
    return np.ascontiguousarray(words), np.ascontiguousarray(byte.astype(np.uint8).reshape(n // 512, 16, m))


K, T, S, N = 512, 2048, 512, 512


def setup_inputs():
    n = np.random.standard_normal
    s = mx_kscale(K)[:, None]
    packed_xT = pack_weight(n((K, T)) * s)
    return {
        "x_words": packed_xT[0],
        "x_scales": packed_xT[1],
        "w1": (n((K, N)) / np.sqrt(K) / s).astype(np.float32),
        "w2": (n((K, N)) / np.sqrt(K) / s).astype(np.float32),
        "offs": striped(np.random.permutation(T)[:S]),
        "ref": striped(np.random.permutation(T)[:S]),
        "c1": striped8(np.stack([np.random.permutation(S) for _ in range(8)])),
        "c2": striped8(np.stack([np.random.permutation(S) for _ in range(8)])),
        "c3": striped8(np.stack([np.random.permutation(S) for _ in range(8)])),
    }


def reference(x_words, x_scales, w1, w2, offs, ref, c1, c2, c3):
    xq = unpack_weight(x_words, x_scales)[:, unstriped(offs)]
    y = mxq(f64(w1), 0, "e4m3").T @ xq
    x_ref = unpack_weight(x_words, x_scales)[:, unstriped(ref)]
    e = mxq(f64(w2), 0, "e4m3").T @ x_ref
    e2 = np.exp(0.25 * (y * (e[np.arange(N)[:, None], runs(c2, N)])))
    e3 = np.exp(0.25 * (y * (e[np.arange(N)[:, None], runs(c3, N)])))
    e1 = np.exp(0.25 * (y * (e[np.arange(N)[:, None], runs(c1, N)])))
    out_0 = (e2 + 2.0 * e3) / (e1 + e2 + e3)
    return (out_0,) + planes(out_0)

@@ -1,0 +1,213 @@
+import math
+from contextlib import ExitStack
+
+import concourse.mybir as mybir
+from concourse.masks import make_identity
+
+K, T, S, N = 512, 2048, 512, 512
+FLOPS = 2 * 2 * K * N * S
+
+F32 = mybir.dt.float32
+BF16 = mybir.dt.bfloat16
+I32 = mybir.dt.int32
+U32 = mybir.dt.uint32
+U16 = mybir.dt.uint16
+U8 = mybir.dt.uint8
+FP8X4 = mybir.dt.float8_e4m3fn_x4
+ACT = mybir.ActivationFunctionType
+ALU = mybir.AluOpType
+
+P = 128
+PACK = 4
+HALVES = 2
+HALF = S // HALVES
+BLOCKS = HALF // P
+W_CHUNKS = 2
+W_COLS = N // W_CHUNKS
+
+SHIFT = 43.5
+UNIT = math.exp(-SHIFT)
+
+
+def tile_picked_softarg_none_po_kernel(tc, x_words, x_scales, w1, w2, offs, ref, c1, c2, c3, out_0, out_1, out_2):
+    nc = tc.nc
+    with ExitStack() as ctx:
+        keep = ctx.enter_context(tc.tile_pool(name="keep", bufs=1))
+        ring = ctx.enter_context(tc.tile_pool(name="ring", bufs=3))
+        psum = ctx.enter_context(tc.psum_pool(name="psum", bufs=2))
+
+        def load_list(src, name):
+            lst = keep.tile([P, S // 16], U16, name=name)
+            nc.sync.dma_start(lst[:], src)
+            return lst
+
+        def load_weight(w, name):
+            chunks = []
+            for c in range(W_CHUNKS):
+                raw = keep.tile([P, PACK, W_COLS], F32, name=f"{name}_raw{c}")
+                nc.sync.dma_start(raw[:], w.rearrange("(p j) n -> p j n", j=PACK)[:, :, c * W_COLS : (c + 1) * W_COLS])
+                chunks.append(raw)
+            return chunks
+
+        table_scales = keep.tile([P, T], U8, name="table_scales", align_bytes=64)
+        nc.vector.memset(table_scales[:].bitcast(I32), 0)
+        for q in range(4):
+            nc.scalar.dma_start(table_scales[32 * q : 32 * q + 4, :].bitcast(I32), x_scales[0][4 * q : 4 * q + 4, :].bitcast(I32))
+
+        ref_list = load_list(ref, "ref_list")
+        table_words = keep.tile([P, T], I32, name="table_words", align_bytes=64)
+        nc.sync.dma_start(table_words[:], x_words[0].rearrange("p n t -> p (n t)").bitcast(I32))
+        offs_list = load_list(offs, "offs_list")
+        w2_raw = load_weight(w2, "w2")
+        w1_raw = load_weight(w1, "w1")
+        c3_list = load_list(c3, "c3_list")
+        c2_list = load_list(c2, "c2_list")
+        c1_list = load_list(c1, "c1_list")
+
+        ident = keep.tile([P, P], F32, name="ident")
+        make_identity(nc, ident[:])
+
+        ones = keep.tile([P, 1], F32, name="ones")
+        nc.gpsimd.memset(ones[:], 1.0)
+
+        def exp_constants():
+            col = keep.tile([P, 2], F32, name="phase")
+            nc.gpsimd.memset(col[:, 0:1], 0.25)
+            nc.gpsimd.memset(col[:, 1:2], -SHIFT)
+            return col
+
+        def log_constants():
+            col = keep.tile([P, 2], F32, name="phase")
+            nc.gpsimd.tensor_scalar(col[:, 0:1], ones[:], UNIT, 0.0, ALU.mult, ALU.add)
+            return col
+
+        warm = keep.tile([P, 1], F32, name="warm")
+        nc.scalar.activation(warm[:], ones[:], ACT.Exp)
+
+        def pick_words(lst, name):
+            words = keep.tile([P, S], U32, name=f"{name}_words", align_bytes=64)
+            nc.vector.tensor_copy(words[:], table_words[:].bitcast(U32).indirect(lst[:]))
+            return words
+
+        def pick_scales(lst, name):
+            scales = keep.tile([P, S], U8, name=f"{name}_scales", align_bytes=64)
+            nc.vector.tensor_copy(scales[:], table_scales[:].indirect(lst[:]))
+            return scales
+
+        def quantize_weight(chunks, copies, name):
+            grouped = keep.tile([P, PACK, P, PACK], BF16, name=f"{name}_bf16", align_bytes=64)
+            per = W_COLS // PACK
+            for c in range(W_CHUNKS):
+                copies[c](
+                    grouped[:, :, c * per : (c + 1) * per, :].rearrange("p t m j -> p m t j"),
+                    chunks[c][:].rearrange("p j (m t) -> p m t j", t=PACK),
+                )
+            planes = []
+            for t in range(PACK):
+                codes = keep.tile([P, P], U32, name=f"{name}_codes{t}", align_bytes=64)
+                scales = keep.tile([P, P], U8, name=f"{name}_scales{t}", align_bytes=64)
+                nc.vector.quantize_mx(out=codes[:].bitcast(FP8X4), scales=scales[:], in_=grouped[:, t, :, :].rearrange("p m j -> p (m j)"))
+                planes.append((codes, scales))
+            return planes
+
+        def project(plane, picked):
+            acc = psum.tile([P, S], F32, name="product", tag="work", bufs=4)
+            nc.tensor.matmul_mx(out=acc[:], lhsT=plane[0][:].bitcast(FP8X4), lhsT_scale=plane[1][:], rhs=picked[0][:].bitcast(FP8X4), rhs_scale=picked[1][:], start=True, stop=True)
+            return acc
+
+        right_words = pick_words(ref_list, "right")
+        left_words = pick_words(offs_list, "left")
+        right = (right_words, pick_scales(ref_list, "right"))
+        left = (left_words, pick_scales(offs_list, "left"))
+        w2_q = quantize_weight(w2_raw, (nc.scalar.copy, nc.scalar.copy), "w2")
+        w1_q = quantize_weight(w1_raw, (nc.scalar.copy, nc.vector.tensor_copy), "w1")
+
+        e_sb, y_pos, y_neg = [], [], []
+        for t in range(PACK):
+            acc = project(w2_q[t], right)
+            e_t = keep.tile([P, S], F32, name=f"e{t}")
+            nc.scalar.copy(e_t[:], acc[:])
+            e_sb.append(e_t)
+            acc = project(w1_q[t], left)
+            neg = keep.tile([P, S], F32, name=f"y_neg{t}")
+            nc.scalar.activation(neg[:], acc[:], ACT.Copy, scale=-1.0)
+            pos = keep.tile([P, S], F32, name=f"y_pos{t}")
+            nc.scalar.copy(pos[:], acc[:])
+            y_neg.append(neg)
+            y_pos.append(pos)
+
+        def add_transposed(dst, parts):
+            for i, part in enumerate(parts):
+                nc.tensor.matmul(dst, part, ident[:], start=(i == 0), stop=(i == len(parts) - 1), is_transpose=True)
+
+        out_rows = out_0.rearrange("(p t) j -> p t j", t=PACK)
+        out_words = out_1[0].rearrange("p n t -> p (n t)").bitcast(I32)
+
+        def finish(h, logs, nums, consts):
+            for b in range(BLOCKS):
+                cols = slice(h * HALF + b * P, h * HALF + (b + 1) * P)
+                inverse = ring.tile([P, PACK * P], F32, name="inverse")
+                nc.scalar.activation(inverse[:], logs[b][:], ACT.Exp, bias=consts[:, 1:2], scale=-1.0)
+                result = keep.tile([P, PACK, P], F32, name=f"result{h}{b}")
+                nc.vector.scalar_tensor_tensor(result[:].rearrange("p t j -> p (t j)"), nums[b][:].rearrange("p t j -> p (t j)"), 2.0, inverse[:], ALU.add, ALU.mult)
+                nc.sync.dma_start(out_rows[:, :, cols], result[:])
+                rounded = keep.tile([P, P, PACK], BF16, name=f"rounded{h}{b}", align_bytes=64)
+                nc.vector.tensor_copy(rounded[:].rearrange("p (c i) t -> p c t i", i=4), result[:].rearrange("p t (c i) -> p c t i", i=4))
+                codes = keep.tile([P, P], U32, name=f"out_codes{h}{b}", align_bytes=64)
+                nc.vector.quantize_mx(out=codes[:].bitcast(FP8X4), scales=out_scales[:, cols], in_=rounded[:].rearrange("p j t -> p (j t)"))
+                nc.sync.dma_start(out_words[:, cols], codes[:].bitcast(I32))
+
+        out_scales = keep.tile([P, S], U8, name="out_scales", align_bytes=64)
+
+        def differences(h, t):
+            cols = slice(h * HALF, (h + 1) * HALF)
+            entries = slice(h * HALF // 16, (h + 1) * HALF // 16)
+            scores = []
+            for lst, factor, name in ((c3_list, y_neg, "s3"), (c2_list, y_pos, "s2"), (c1_list, y_pos, "s1")):
+                sc = keep.tile([P, HALF], F32, name=f"{name}_{h}{t}")
+                nc.vector.tensor_tensor(sc[:], e_sb[t][:].indirect(lst[:, entries]), factor[t][:, cols], ALU.mult)
+                scores.append(sc)
+            diff = psum.tile([P, 2 * HALF], F32, name="diff", tag="work", bufs=4)
+            for i in range(2):
+                for b in range(BLOCKS):
+                    blk = slice(b * P, (b + 1) * P)
+                    add_transposed(diff[:, i * HALF + b * P : i * HALF + (b + 1) * P], [scores[0][:, blk], scores[1 + i][:, blk]])
+            return diff
+
+        def exponentiate(h, t, diff, consts):
+            ratio = keep.tile([P, 2, BLOCKS, P], F32, name=f"ratio{h}{t}")
+            nc.scalar.activation(ratio[:].rearrange("p i b m -> p (i b m)"), diff[:], ACT.Exp, scale=consts[:, 0:1])
+            return ratio
+
+        def sum_back(ratios, name, terms):
+            banks = [psum.tile([P, PACK, P], F32, name=name) for b in range(BLOCKS)]
+            for t in range(PACK):
+                for b in range(BLOCKS):
+                    add_transposed(banks[b][:, t, :], [ratios[t][:, i, b, :] for i in range(terms)])
+            return banks
+
+        def take_logs(dens):
+            floor = log_constants()
+            logs = []
+            for b in range(BLOCKS):
+                log_den = ring.tile([P, PACK * P], F32, name="log_den")
+                nc.scalar.activation(log_den[:], dens[b][:].rearrange("p t j -> p (t j)"), ACT.Ln, bias=floor[:, 0:1], scale=UNIT)
+                logs.append(log_den)
+            return logs
+
+        consts = exp_constants()
+        ratios = [exponentiate(0, t, differences(0, t), consts) for t in range(PACK)]
+        dens = sum_back(ratios, "den", 2)
+        nums_first = sum_back(ratios, "num", 1)
+        logs_first = take_logs(dens)
+        diffs = [differences(1, t) for t in range(PACK)]
+        consts = exp_constants()
+        ratios = [exponentiate(1, t, diffs[t], consts) for t in range(PACK)]
+        dens = sum_back(ratios, "den", 2)
+        finish(0, logs_first, nums_first, consts)
+        nums_second = sum_back(ratios, "num", 1)
+        logs_second = take_logs(dens)
+        finish(1, logs_second, nums_second, exp_constants())
+        for q in range(4):
+            queue = nc.scalar if q % 2 else nc.sync
+            queue.dma_start(out_2[0][4 * q : 4 * q + 4, :].bitcast(I32), out_scales[32 * q : 32 * q + 4, :].bitcast(I32))

@@ -19,11 +19,14 @@ ALU = mybir.AluOpType
 
 P = 128
 PACK = 4
-HALVES = 2
-HALF = S // HALVES
+QUADRANTS = 4
+ENTRIES = 16
+HALF = S // 2
 BLOCKS = HALF // P
-W_CHUNKS = 2
-W_COLS = N // W_CHUNKS
+W_COLS = N // 2
+TURNED = 2
+PLAIN = PACK - TURNED
+BANK_BYTES = 2048
 
 SHIFT = 43.5
 UNIT = math.exp(-SHIFT)
@@ -33,30 +36,37 @@ def tile_picked_softarg_none_po_kernel(tc, x_words, x_scales, w1, w2, offs, ref,
     nc = tc.nc
     with ExitStack() as ctx:
         keep = ctx.enter_context(tc.tile_pool(name="keep", bufs=1))
-        ring = ctx.enter_context(tc.tile_pool(name="ring", bufs=3))
-        psum = ctx.enter_context(tc.psum_pool(name="psum", bufs=2))
+        reuse = ctx.enter_context(tc.tile_pool(name="reuse", bufs=1))
+        psum = ctx.enter_context(tc.psum_pool(name="psum", bufs=1))
 
-        def load_list(src, name):
-            lst = keep.tile([P, S // 16], U16, name=name)
-            nc.sync.dma_start(lst[:], src)
-            return lst
+        def in_bank(bank, shape, name):
+            return psum.tile(shape, F32, name=name, offset=bank * BANK_BYTES)
 
-        def load_weight(w, name):
-            chunks = []
-            for c in range(W_CHUNKS):
-                raw = keep.tile([P, PACK, W_COLS], F32, name=f"{name}_raw{c}")
-                nc.sync.dma_start(raw[:], w.rearrange("(p j) n -> p j n", j=PACK)[:, :, c * W_COLS : (c + 1) * W_COLS])
-                chunks.append(raw)
-            return chunks
-
+        staged_scales = keep.tile([P, T // 4], I32, name="staged_scales")
+        for q in range(QUADRANTS):
+            queue = nc.scalar if q % 2 else nc.sync
+            queue.dma_start(staged_scales[32 * q : 32 * q + 4, :], x_scales[0][4 * q : 4 * q + 4, :].bitcast(I32))
         table_scales = keep.tile([P, T], U8, name="table_scales", align_bytes=64)
         nc.vector.memset(table_scales[:].bitcast(I32), 0)
-        for q in range(4):
-            nc.scalar.dma_start(table_scales[32 * q : 32 * q + 4, :].bitcast(I32), x_scales[0][4 * q : 4 * q + 4, :].bitcast(I32))
+        for q in range(QUADRANTS):
+            nc.vector.tensor_copy(table_scales[32 * q : 32 * q + 4, :].bitcast(I32), staged_scales[32 * q : 32 * q + 4, :])
 
-        ref_list = load_list(ref, "ref_list")
+        def load_list(source, name):
+            offsets = keep.tile([P, S // ENTRIES], U16, name=name)
+            nc.sync.dma_start(offsets[:], source)
+            return offsets
+
+        def load_weight(w, name):
+            pieces = []
+            for c in range(N // W_COLS):
+                raw = keep.tile([P, PACK, W_COLS], F32, name=f"{name}_raw{c}", align_bytes=64)
+                nc.sync.dma_start(raw[:], w.rearrange("(p r) n -> p r n", r=PACK)[:, :, c * W_COLS : (c + 1) * W_COLS])
+                pieces.append(raw)
+            return pieces
+
         table_words = keep.tile([P, T], I32, name="table_words", align_bytes=64)
-        nc.sync.dma_start(table_words[:], x_words[0].rearrange("p n t -> p (n t)").bitcast(I32))
+        nc.sync.dma_start(table_words[:], x_words[0].rearrange("p n r -> p (n r)").bitcast(I32))
+        ref_list = load_list(ref, "ref_list")
         offs_list = load_list(offs, "offs_list")
         w2_raw = load_weight(w2, "w2")
         w1_raw = load_weight(w1, "w1")
@@ -64,150 +74,192 @@ def tile_picked_softarg_none_po_kernel(tc, x_words, x_scales, w1, w2, offs, ref,
         c2_list = load_list(c2, "c2_list")
         c1_list = load_list(c1, "c1_list")
 
-        ident = keep.tile([P, P], F32, name="ident")
-        make_identity(nc, ident[:])
-
+        identity = keep.tile([P, P], F32, name="identity")
+        make_identity(nc, identity[:])
         ones = keep.tile([P, 1], F32, name="ones")
         nc.gpsimd.memset(ones[:], 1.0)
+        minus_shift = keep.tile([P, 1], F32, name="minus_shift")
+        nc.gpsimd.memset(minus_shift[:], -SHIFT)
+        plus_shift = keep.tile([P, 1], F32, name="plus_shift")
+        nc.scalar.activation(plus_shift[:], ones[:], ACT.Copy, scale=SHIFT)
 
-        def exp_constants():
-            col = keep.tile([P, 2], F32, name="phase")
-            nc.gpsimd.memset(col[:, 0:1], 0.25)
-            nc.gpsimd.memset(col[:, 1:2], -SHIFT)
-            return col
+        def exp_scale():
+            column = keep.tile([P, 2], F32, name="stretch")
+            nc.gpsimd.memset(column[:, 0:1], 0.25)
+            return column[:, 0:1]
 
-        def log_constants():
-            col = keep.tile([P, 2], F32, name="phase")
-            nc.gpsimd.tensor_scalar(col[:, 0:1], ones[:], UNIT, 0.0, ALU.mult, ALU.add)
-            return col
+        def ln_biases():
+            columns = keep.tile([P, 2], F32, name="stretch")
+            nc.gpsimd.tensor_scalar(columns[:, 0:1], ones[:], UNIT, 0.0, ALU.mult, ALU.add)
+            nc.gpsimd.memset(columns[:, 1:2], 0.0)
+            return columns[:, 0:1], columns[:, 1:2]
 
-        warm = keep.tile([P, 1], F32, name="warm")
-        nc.scalar.activation(warm[:], ones[:], ACT.Exp)
+        def half_of(offsets, h):
+            return offsets[:, h * HALF // ENTRIES : (h + 1) * HALF // ENTRIES]
 
-        def pick_words(lst, name):
-            words = keep.tile([P, S], U32, name=f"{name}_words", align_bytes=64)
-            nc.vector.tensor_copy(words[:], table_words[:].bitcast(U32).indirect(lst[:]))
-            return words
+        def pick_words(offsets, picked):
+            nc.vector.tensor_copy(picked[:], table_words[:].bitcast(U32).indirect(offsets))
+            return picked[:]
 
-        def pick_scales(lst, name):
-            scales = keep.tile([P, S], U8, name=f"{name}_scales", align_bytes=64)
-            nc.vector.tensor_copy(scales[:], table_scales[:].indirect(lst[:]))
-            return scales
+        def pick_scales(offsets, picked):
+            nc.vector.tensor_copy(picked[:], table_scales[:].indirect(offsets))
+            return picked[:]
 
-        def quantize_weight(chunks, copies, name):
-            grouped = keep.tile([P, PACK, P, PACK], BF16, name=f"{name}_bf16", align_bytes=64)
-            per = W_COLS // PACK
-            for c in range(W_CHUNKS):
-                copies[c](
-                    grouped[:, :, c * per : (c + 1) * per, :].rearrange("p t m j -> p m t j"),
-                    chunks[c][:].rearrange("p j (m t) -> p m t j", t=PACK),
+        def quantize_weight(pieces, copies, grouped, name):
+            per_piece = W_COLS // PACK
+            for c, copy in enumerate(copies):
+                copy(
+                    grouped[:, :, c * per_piece : (c + 1) * per_piece, :].rearrange("p t m r -> p m t r"),
+                    pieces[c][:].rearrange("p r (m t) -> p m t r", t=PACK),
                 )
-            planes = []
+            slices = []
             for t in range(PACK):
                 codes = keep.tile([P, P], U32, name=f"{name}_codes{t}", align_bytes=64)
                 scales = keep.tile([P, P], U8, name=f"{name}_scales{t}", align_bytes=64)
-                nc.vector.quantize_mx(out=codes[:].bitcast(FP8X4), scales=scales[:], in_=grouped[:, t, :, :].rearrange("p m j -> p (m j)"))
-                planes.append((codes, scales))
-            return planes
+                nc.vector.quantize_mx(out=codes[:].bitcast(FP8X4), scales=scales[:], in_=grouped[:, t, :, :].rearrange("p m r -> p (m r)"))
+                slices.append((codes, scales))
+            return slices
 
-        def project(plane, picked):
-            acc = psum.tile([P, S], F32, name="product", tag="work", bufs=4)
-            nc.tensor.matmul_mx(out=acc[:], lhsT=plane[0][:].bitcast(FP8X4), lhsT_scale=plane[1][:], rhs=picked[0][:].bitcast(FP8X4), rhs_scale=picked[1][:], start=True, stop=True)
-            return acc
+        right_words = pick_words(ref_list[:], keep.tile([P, S], U32, name="right_words", align_bytes=64))
+        left_words = pick_words(half_of(offs_list, 0), keep.tile([P, HALF], U32, name="left0_words", align_bytes=64))
+        right = (right_words, pick_scales(ref_list[:], keep.tile([P, S], U8, name="right_scales", align_bytes=64)))
+        left = [(left_words, pick_scales(half_of(offs_list, 0), keep.tile([P, HALF], U8, name="left0_scales", align_bytes=64)))]
+        w2_bf16 = keep.tile([P, PACK, P, PACK], BF16, name="w2_bf16", align_bytes=64)
+        w2_slices = quantize_weight(w2_raw, (nc.scalar.copy, nc.scalar.copy), w2_bf16, "w2")
+        w1_bf16 = reuse.tile([P, PACK, P, PACK], BF16, name="w1_bf16", align_bytes=64, offset=0)
+        w1_slices = quantize_weight(w1_raw, (nc.scalar.copy, nc.vector.tensor_copy), w1_bf16, "w1")
+        left.append(
+            (
+                pick_words(half_of(offs_list, 1), reuse.tile([P, HALF], U32, name="left1_words", align_bytes=64, offset=0)),
+                pick_scales(half_of(offs_list, 1), reuse.tile([P, HALF], U8, name="left1_scales", align_bytes=64, offset=4 * HALF)),
+            )
+        )
 
-        right_words = pick_words(ref_list, "right")
-        left_words = pick_words(offs_list, "left")
-        right = (right_words, pick_scales(ref_list, "right"))
-        left = (left_words, pick_scales(offs_list, "left"))
-        w2_q = quantize_weight(w2_raw, (nc.scalar.copy, nc.scalar.copy), "w2")
-        w1_q = quantize_weight(w1_raw, (nc.scalar.copy, nc.vector.tensor_copy), "w1")
+        def project(acc, weight, picked):
+            nc.tensor.matmul_mx(
+                out=acc, lhsT=weight[0][:].bitcast(FP8X4), lhsT_scale=weight[1][:], rhs=picked[0].bitcast(FP8X4), rhs_scale=picked[1], start=True, stop=True
+            )
 
-        e_sb, y_pos, y_neg = [], [], []
-        for t in range(PACK):
-            acc = project(w2_q[t], right)
-            e_t = keep.tile([P, S], F32, name=f"e{t}")
-            nc.scalar.copy(e_t[:], acc[:])
-            e_sb.append(e_t)
-            acc = project(w1_q[t], left)
-            neg = keep.tile([P, S], F32, name=f"y_neg{t}")
-            nc.scalar.activation(neg[:], acc[:], ACT.Copy, scale=-1.0)
-            pos = keep.tile([P, S], F32, name=f"y_pos{t}")
-            nc.scalar.copy(pos[:], acc[:])
-            y_neg.append(neg)
-            y_pos.append(pos)
+        e, y, minus_y = {}, {}, {}
 
-        def add_transposed(dst, parts):
+        def project_right(t, bank):
+            acc = in_bank(bank, [P, S], f"right{t}")
+            project(acc[:], w2_slices[t], right)
+            e[t] = keep.tile([P, S], F32, name=f"e{t}")
+            nc.scalar.copy(e[t][:], acc[:])
+
+        def project_left(h, slices, bank):
+            acc = in_bank(bank, [P, len(slices), HALF], f"left{h}{slices[0]}")
+            for i, t in enumerate(slices):
+                project(acc[:, i, :], w1_slices[t], left[h])
+            if slices[0] < TURNED:
+                negated = keep.tile([P, len(slices), HALF], F32, name=f"minus_y{h}{slices[0]}")
+                nc.scalar.activation(negated[:], acc[:], ACT.Copy, scale=-1.0)
+                for i, t in enumerate(slices):
+                    minus_y[h, t] = negated[:, i, :]
+            copied = keep.tile([P, len(slices), HALF], F32, name=f"y{h}{slices[0]}")
+            nc.scalar.copy(copied[:], acc[:])
+            for i, t in enumerate(slices):
+                y[h, t] = copied[:, i, :]
+
+        DIFFERENCE_BANK, SUM_BANK, NUMERATOR_BANK = 0, 4, (6, 2)
+        project_right(0, 4)
+        project_left(0, [0], 0)
+        project_right(1, 5)
+        project_left(0, [1], 1)
+        project_right(2, 6)
+        project_left(0, [2, 3], 2)
+        project_right(3, 7)
+        project_left(1, [0, 1], 3)
+        project_left(1, [2, 3], 6)
+
+        def add_turned(target, parts):
             for i, part in enumerate(parts):
-                nc.tensor.matmul(dst, part, ident[:], start=(i == 0), stop=(i == len(parts) - 1), is_transpose=True)
+                nc.tensor.matmul(target, part, identity[:], start=(i == 0), stop=(i == len(parts) - 1), is_transpose=True)
 
-        out_rows = out_0.rearrange("(p t) j -> p t j", t=PACK)
-        out_words = out_1[0].rearrange("p n t -> p (n t)").bitcast(I32)
-
-        def finish(h, logs, nums, consts):
-            for b in range(BLOCKS):
-                cols = slice(h * HALF + b * P, h * HALF + (b + 1) * P)
-                inverse = ring.tile([P, PACK * P], F32, name="inverse")
-                nc.scalar.activation(inverse[:], logs[b][:], ACT.Exp, bias=consts[:, 1:2], scale=-1.0)
-                result = keep.tile([P, PACK, P], F32, name=f"result{h}{b}")
-                nc.vector.scalar_tensor_tensor(result[:].rearrange("p t j -> p (t j)"), nums[b][:].rearrange("p t j -> p (t j)"), 2.0, inverse[:], ALU.add, ALU.mult)
-                nc.sync.dma_start(out_rows[:, :, cols], result[:])
-                rounded = keep.tile([P, P, PACK], BF16, name=f"rounded{h}{b}", align_bytes=64)
-                nc.vector.tensor_copy(rounded[:].rearrange("p (c i) t -> p c t i", i=4), result[:].rearrange("p t (c i) -> p c t i", i=4))
-                codes = keep.tile([P, P], U32, name=f"out_codes{h}{b}", align_bytes=64)
-                nc.vector.quantize_mx(out=codes[:].bitcast(FP8X4), scales=out_scales[:, cols], in_=rounded[:].rearrange("p j t -> p (j t)"))
-                nc.sync.dma_start(out_words[:, cols], codes[:].bitcast(I32))
-
-        out_scales = keep.tile([P, S], U8, name="out_scales", align_bytes=64)
-
-        def differences(h, t):
-            cols = slice(h * HALF, (h + 1) * HALF)
-            entries = slice(h * HALF // 16, (h + 1) * HALF // 16)
-            scores = []
-            for lst, factor, name in ((c3_list, y_neg, "s3"), (c2_list, y_pos, "s2"), (c1_list, y_pos, "s1")):
-                sc = keep.tile([P, HALF], F32, name=f"{name}_{h}{t}")
-                nc.vector.tensor_tensor(sc[:], e_sb[t][:].indirect(lst[:, entries]), factor[t][:, cols], ALU.mult)
-                scores.append(sc)
-            diff = psum.tile([P, 2 * HALF], F32, name="diff", tag="work", bufs=4)
-            for i in range(2):
-                for b in range(BLOCKS):
-                    blk = slice(b * P, (b + 1) * P)
-                    add_transposed(diff[:, i * HALF + b * P : i * HALF + (b + 1) * P], [scores[0][:, blk], scores[1 + i][:, blk]])
-            return diff
-
-        def exponentiate(h, t, diff, consts):
-            ratio = keep.tile([P, 2, BLOCKS, P], F32, name=f"ratio{h}{t}")
-            nc.scalar.activation(ratio[:].rearrange("p i b m -> p (i b m)"), diff[:], ACT.Exp, scale=consts[:, 0:1])
-            return ratio
-
-        def sum_back(ratios, name, terms):
-            banks = [psum.tile([P, PACK, P], F32, name=name) for b in range(BLOCKS)]
+        def look_up(h, products):
+            differences = []
             for t in range(PACK):
-                for b in range(BLOCKS):
-                    add_transposed(banks[b][:, t, :], [ratios[t][:, i, b, :] for i in range(terms)])
-            return banks
+                for i, (offsets, factor) in enumerate(((c3_list, minus_y if t < TURNED else y), (c2_list, y), (c1_list, y))):
+                    nc.vector.tensor_tensor(products[:, t, i, :], e[t][:].indirect(half_of(offsets, h)), factor[h, t], ALU.mult)
+                if t < TURNED:
+                    difference = in_bank(DIFFERENCE_BANK + t, [P, 2, BLOCKS, P], f"difference{h}{t}")
+                    for i in range(2):
+                        for b in range(BLOCKS):
+                            block = slice(b * P, (b + 1) * P)
+                            add_turned(difference[:, i, b, :], [products[:, t, 0, block], products[:, t, 1 + i, block]])
+                    differences.append(difference)
+            return differences
 
-        def take_logs(dens):
-            floor = log_constants()
-            logs = []
+        def exponentiate(h, products, differences):
+            quarter = exp_scale()
+            sums = [in_bank(SUM_BANK + b, [P, TURNED, P], f"sum{h}{b}") for b in range(BLOCKS)]
+            numerators = [in_bank(NUMERATOR_BANK[h] + b, [P, TURNED, P], f"numerator{h}{b}") for b in range(BLOCKS)]
+            for t in range(TURNED):
+                ratios = keep.tile([P, 2, BLOCKS, P], F32, name=f"ratios{h}{t}")
+                nc.scalar.activation(ratios[:], differences[t][:], ACT.Exp, scale=quarter)
+                for b in range(BLOCKS):
+                    add_turned(sums[b][:, t, :], [ratios[:, 0, b, :], ratios[:, 1, b, :]])
+                for b in range(BLOCKS):
+                    add_turned(numerators[b][:, t, :], [ratios[:, 0, b, :]])
+            weights = keep.tile([P, 3, BLOCKS, PLAIN, P], F32, name=f"weights{h}")
+            for t in range(TURNED, PACK):
+                for lists in (slice(0, 2), slice(2, 3)) if t == PACK - 1 else (slice(0, 3),):
+                    nc.scalar.activation(
+                        weights[:, lists, :, t - TURNED, :], products[:, t, lists, :].rearrange("p i (b j) -> p i b j", b=BLOCKS), ACT.Exp, bias=plus_shift[:], scale=quarter
+                    )
+            by_list = weights[:].rearrange("p i b t j -> p i (b t j)")
+            pair = keep.tile([P, PLAIN * HALF], F32, name=f"pair{h}")
+            nc.vector.tensor_tensor(pair[:], by_list[:, 0, :], by_list[:, 1, :], ALU.add)
+            total = keep.tile([P, BLOCKS, PLAIN * P], F32, name=f"total{h}")
+            nc.vector.tensor_tensor(total[:].rearrange("p b n -> p (b n)"), pair[:], by_list[:, 2, :], ALU.add)
+            return sums, numerators, by_list, total
+
+        def take_logs(h, sums, total):
+            turned_bias, plain_bias = ln_biases()
+            logs = keep.tile([P, BLOCKS, PACK * P], F32, name=f"logs{h}")
             for b in range(BLOCKS):
-                log_den = ring.tile([P, PACK * P], F32, name="log_den")
-                nc.scalar.activation(log_den[:], dens[b][:].rearrange("p t j -> p (t j)"), ACT.Ln, bias=floor[:, 0:1], scale=UNIT)
-                logs.append(log_den)
+                nc.scalar.activation(logs[:, b, : TURNED * P], sums[b][:].rearrange("p t j -> p (t j)"), ACT.Ln, bias=turned_bias, scale=UNIT)
+            nc.scalar.activation(logs[:, :, TURNED * P :], total[:], ACT.Ln, bias=plain_bias, scale=UNIT)
             return logs
 
-        consts = exp_constants()
-        ratios = [exponentiate(0, t, differences(0, t), consts) for t in range(PACK)]
-        dens = sum_back(ratios, "den", 2)
-        nums_first = sum_back(ratios, "num", 1)
-        logs_first = take_logs(dens)
-        diffs = [differences(1, t) for t in range(PACK)]
-        consts = exp_constants()
-        ratios = [exponentiate(1, t, diffs[t], consts) for t in range(PACK)]
-        dens = sum_back(ratios, "den", 2)
-        finish(0, logs_first, nums_first, consts)
-        nums_second = sum_back(ratios, "num", 1)
-        logs_second = take_logs(dens)
-        finish(1, logs_second, nums_second, exp_constants())
-        for q in range(4):
+        def invert(h, logs):
+            inverses = []
+            for b in range(BLOCKS):
+                inverse = keep.tile([P, PACK * P], F32, name=f"inverse{h}{b}")
+                nc.scalar.activation(inverse[:], logs[:, b, :], ACT.Exp, bias=minus_shift[:], scale=-1.0)
+                inverses.append(inverse)
+            return inverses
+
+        out_rows = out_0.rearrange("(p t) j -> p t j", t=PACK)
+        out_words = out_1[0].rearrange("p n r -> p (n r)").bitcast(I32)
+        out_scales = keep.tile([P, S], U8, name="out_scales", align_bytes=64)
+
+        def finish(h, inverses, numerators, by_list, weighted):
+            nc.vector.scalar_tensor_tensor(weighted[:], by_list[:, 0, :], 2.0, by_list[:, 1, :], ALU.mult, ALU.add)
+            for b in range(BLOCKS):
+                columns = slice(h * HALF + b * P, h * HALF + (b + 1) * P)
+                result = keep.tile([P, PACK * P], F32, name=f"result{h}{b}")
+                nc.vector.scalar_tensor_tensor(
+                    result[:, : TURNED * P], numerators[b][:].rearrange("p t j -> p (t j)"), 2.0, inverses[b][:, : TURNED * P], ALU.add, ALU.mult
+                )
+                nc.vector.tensor_tensor(result[:, TURNED * P :], weighted[:, b * PLAIN * P : (b + 1) * PLAIN * P], inverses[b][:, TURNED * P :], ALU.mult)
+                nc.sync.dma_start(out_rows[:, :, columns], result[:].rearrange("p (t j) -> p t j", t=PACK))
+                rounded = keep.tile([P, P, PACK], BF16, name=f"rounded{h}{b}", align_bytes=64)
+                nc.vector.tensor_copy(rounded[:].rearrange("p (c i) t -> p c t i", i=4), result[:].rearrange("p (t c i) -> p c t i", t=PACK, i=4))
+                codes = keep.tile([P, P], U32, name=f"out_codes{h}{b}", align_bytes=64)
+                nc.vector.quantize_mx(out=codes[:].bitcast(FP8X4), scales=out_scales[:, columns], in_=rounded[:].rearrange("p j t -> p (j t)"))
+                nc.sync.dma_start(out_words[:, columns], codes[:].bitcast(I32))
+
+        products = keep.tile([P, PACK, 3, HALF], F32, name="products0")
+        sums, first_numerators, first_by_list, total = exponentiate(0, products, look_up(0, products))
+        first_logs = take_logs(0, sums, total)
+        products = keep.tile([P, PACK, 3, HALF], F32, name="products1", tag="pair0")
+        differences = look_up(1, products)
+        first_inverses = invert(0, first_logs)
+        sums, numerators, by_list, total = exponentiate(1, products, differences)
+        finish(0, first_inverses, first_numerators, first_by_list, keep.tile([P, PLAIN * HALF], F32, name="weighted0", tag="pair1"))
+        finish(1, invert(1, take_logs(1, sums, total)), numerators, by_list, keep.tile([P, PLAIN * HALF], F32, name="weighted1"))
+        for q in range(QUADRANTS):
             queue = nc.scalar if q % 2 else nc.sync
             queue.dma_start(out_2[0][4 * q : 4 * q + 4, :].bitcast(I32), out_scales[32 * q : 32 * q + 4, :].bitcast(I32))

import math
from contextlib import ExitStack

import concourse.mybir as mybir
from concourse.masks import make_identity

K, T, S, N = 512, 2048, 512, 512
FLOPS = 2 * 2 * K * N * S

F32 = mybir.dt.float32
BF16 = mybir.dt.bfloat16
I32 = mybir.dt.int32
U32 = mybir.dt.uint32
U16 = mybir.dt.uint16
U8 = mybir.dt.uint8
FP8X4 = mybir.dt.float8_e4m3fn_x4
ACT = mybir.ActivationFunctionType
ALU = mybir.AluOpType

P = 128
PACK = 4
QUADRANTS = 4
ENTRIES = 16
HALF = S // 2
BLOCKS = HALF // P
W_COLS = N // 2
TURNED = 2
PLAIN = PACK - TURNED
BANK_BYTES = 2048

SHIFT = 43.5
UNIT = math.exp(-SHIFT)


def tile_picked_softarg_none_po_kernel(tc, x_words, x_scales, w1, w2, offs, ref, c1, c2, c3, out_0, out_1, out_2):
    nc = tc.nc
    with ExitStack() as ctx:
        keep = ctx.enter_context(tc.tile_pool(name="keep", bufs=1))
        reuse = ctx.enter_context(tc.tile_pool(name="reuse", bufs=1))
        psum = ctx.enter_context(tc.psum_pool(name="psum", bufs=1))

        def in_bank(bank, shape, name):
            return psum.tile(shape, F32, name=name, offset=bank * BANK_BYTES)

        staged_scales = keep.tile([P, T // 4], I32, name="staged_scales")
        for q in range(QUADRANTS):
            queue = nc.scalar if q % 2 else nc.sync
            queue.dma_start(staged_scales[32 * q : 32 * q + 4, :], x_scales[0][4 * q : 4 * q + 4, :].bitcast(I32))
        table_scales = keep.tile([P, T], U8, name="table_scales", align_bytes=64)
        nc.vector.memset(table_scales[:].bitcast(I32), 0)
        for q in range(QUADRANTS):
            nc.vector.tensor_copy(table_scales[32 * q : 32 * q + 4, :].bitcast(I32), staged_scales[32 * q : 32 * q + 4, :])

        def load_list(source, name):
            offsets = keep.tile([P, S // ENTRIES], U16, name=name)
            nc.sync.dma_start(offsets[:], source)
            return offsets

        def load_weight(w, name):
            pieces = []
            for c in range(N // W_COLS):
                raw = keep.tile([P, PACK, W_COLS], F32, name=f"{name}_raw{c}", align_bytes=64)
                nc.sync.dma_start(raw[:], w.rearrange("(p r) n -> p r n", r=PACK)[:, :, c * W_COLS : (c + 1) * W_COLS])
                pieces.append(raw)
            return pieces

        table_words = keep.tile([P, T], I32, name="table_words", align_bytes=64)
        nc.sync.dma_start(table_words[:], x_words[0].rearrange("p n r -> p (n r)").bitcast(I32))
        ref_list = load_list(ref, "ref_list")
        offs_list = load_list(offs, "offs_list")
        w2_raw = load_weight(w2, "w2")
        w1_raw = load_weight(w1, "w1")
        c3_list = load_list(c3, "c3_list")
        c2_list = load_list(c2, "c2_list")
        c1_list = load_list(c1, "c1_list")

        identity = keep.tile([P, P], F32, name="identity")
        make_identity(nc, identity[:])
        ones = keep.tile([P, 1], F32, name="ones")
        nc.gpsimd.memset(ones[:], 1.0)
        minus_shift = keep.tile([P, 1], F32, name="minus_shift")
        nc.gpsimd.memset(minus_shift[:], -SHIFT)
        plus_shift = keep.tile([P, 1], F32, name="plus_shift")
        nc.scalar.activation(plus_shift[:], ones[:], ACT.Copy, scale=SHIFT)

        def exp_scale():
            column = keep.tile([P, 2], F32, name="stretch")
            nc.gpsimd.memset(column[:, 0:1], 0.25)
            return column[:, 0:1]

        def ln_biases():
            columns = keep.tile([P, 2], F32, name="stretch")
            nc.gpsimd.tensor_scalar(columns[:, 0:1], ones[:], UNIT, 0.0, ALU.mult, ALU.add)
            nc.gpsimd.memset(columns[:, 1:2], 0.0)
            return columns[:, 0:1], columns[:, 1:2]

        def half_of(offsets, h):
            return offsets[:, h * HALF // ENTRIES : (h + 1) * HALF // ENTRIES]

        def pick_words(offsets, picked):
            nc.vector.tensor_copy(picked[:], table_words[:].bitcast(U32).indirect(offsets))
            return picked[:]

        def pick_scales(offsets, picked):
            nc.vector.tensor_copy(picked[:], table_scales[:].indirect(offsets))
            return picked[:]

        def quantize_weight(pieces, copies, grouped, name):
            per_piece = W_COLS // PACK
            for c, copy in enumerate(copies):
                copy(
                    grouped[:, :, c * per_piece : (c + 1) * per_piece, :].rearrange("p t m r -> p m t r"),
                    pieces[c][:].rearrange("p r (m t) -> p m t r", t=PACK),
                )
            slices = []
            for t in range(PACK):
                codes = keep.tile([P, P], U32, name=f"{name}_codes{t}", align_bytes=64)
                scales = keep.tile([P, P], U8, name=f"{name}_scales{t}", align_bytes=64)
                nc.vector.quantize_mx(out=codes[:].bitcast(FP8X4), scales=scales[:], in_=grouped[:, t, :, :].rearrange("p m r -> p (m r)"))
                slices.append((codes, scales))
            return slices

        right_words = pick_words(ref_list[:], keep.tile([P, S], U32, name="right_words", align_bytes=64))
        left_words = pick_words(half_of(offs_list, 0), keep.tile([P, HALF], U32, name="left0_words", align_bytes=64))
        right = (right_words, pick_scales(ref_list[:], keep.tile([P, S], U8, name="right_scales", align_bytes=64)))
        left = [(left_words, pick_scales(half_of(offs_list, 0), keep.tile([P, HALF], U8, name="left0_scales", align_bytes=64)))]
        w2_bf16 = keep.tile([P, PACK, P, PACK], BF16, name="w2_bf16", align_bytes=64)
        w2_slices = quantize_weight(w2_raw, (nc.scalar.copy, nc.scalar.copy), w2_bf16, "w2")
        w1_bf16 = reuse.tile([P, PACK, P, PACK], BF16, name="w1_bf16", align_bytes=64, offset=0)
        w1_slices = quantize_weight(w1_raw, (nc.scalar.copy, nc.vector.tensor_copy), w1_bf16, "w1")
        left.append(
            (
                pick_words(half_of(offs_list, 1), reuse.tile([P, HALF], U32, name="left1_words", align_bytes=64, offset=0)),
                pick_scales(half_of(offs_list, 1), reuse.tile([P, HALF], U8, name="left1_scales", align_bytes=64, offset=4 * HALF)),
            )
        )

        def project(acc, weight, picked):
            nc.tensor.matmul_mx(
                out=acc, lhsT=weight[0][:].bitcast(FP8X4), lhsT_scale=weight[1][:], rhs=picked[0].bitcast(FP8X4), rhs_scale=picked[1], start=True, stop=True
            )

        e, y, minus_y = {}, {}, {}

        def project_right(t, bank):
            acc = in_bank(bank, [P, S], f"right{t}")
            project(acc[:], w2_slices[t], right)
            e[t] = keep.tile([P, S], F32, name=f"e{t}")
            nc.scalar.copy(e[t][:], acc[:])

        def project_left(h, slices, bank):
            acc = in_bank(bank, [P, len(slices), HALF], f"left{h}{slices[0]}")
            for i, t in enumerate(slices):
                project(acc[:, i, :], w1_slices[t], left[h])
            if slices[0] < TURNED:
                negated = keep.tile([P, len(slices), HALF], F32, name=f"minus_y{h}{slices[0]}")
                nc.scalar.activation(negated[:], acc[:], ACT.Copy, scale=-1.0)
                for i, t in enumerate(slices):
                    minus_y[h, t] = negated[:, i, :]
            copied = keep.tile([P, len(slices), HALF], F32, name=f"y{h}{slices[0]}")
            nc.scalar.copy(copied[:], acc[:])
            for i, t in enumerate(slices):
                y[h, t] = copied[:, i, :]

        DIFFERENCE_BANK, SUM_BANK, NUMERATOR_BANK = 0, 4, (6, 2)
        project_right(0, 4)
        project_left(0, [0], 0)
        project_right(1, 5)
        project_left(0, [1], 1)
        project_right(2, 6)
        project_left(0, [2, 3], 2)
        project_right(3, 7)
        project_left(1, [0, 1], 3)
        project_left(1, [2, 3], 6)

        def add_turned(target, parts):
            for i, part in enumerate(parts):
                nc.tensor.matmul(target, part, identity[:], start=(i == 0), stop=(i == len(parts) - 1), is_transpose=True)

        def look_up(h, products):
            differences = []
            for t in range(PACK):
                for i, (offsets, factor) in enumerate(((c3_list, minus_y if t < TURNED else y), (c2_list, y), (c1_list, y))):
                    nc.vector.tensor_tensor(products[:, t, i, :], e[t][:].indirect(half_of(offsets, h)), factor[h, t], ALU.mult)
                if t < TURNED:
                    difference = in_bank(DIFFERENCE_BANK + t, [P, 2, BLOCKS, P], f"difference{h}{t}")
                    for i in range(2):
                        for b in range(BLOCKS):
                            block = slice(b * P, (b + 1) * P)
                            add_turned(difference[:, i, b, :], [products[:, t, 0, block], products[:, t, 1 + i, block]])
                    differences.append(difference)
            return differences

        def exponentiate(h, products, differences):
            quarter = exp_scale()
            sums = [in_bank(SUM_BANK + b, [P, TURNED, P], f"sum{h}{b}") for b in range(BLOCKS)]
            numerators = [in_bank(NUMERATOR_BANK[h] + b, [P, TURNED, P], f"numerator{h}{b}") for b in range(BLOCKS)]
            for t in range(TURNED):
                ratios = keep.tile([P, 2, BLOCKS, P], F32, name=f"ratios{h}{t}")
                nc.scalar.activation(ratios[:], differences[t][:], ACT.Exp, scale=quarter)
                for b in range(BLOCKS):
                    add_turned(sums[b][:, t, :], [ratios[:, 0, b, :], ratios[:, 1, b, :]])
                for b in range(BLOCKS):
                    add_turned(numerators[b][:, t, :], [ratios[:, 0, b, :]])
            weights = keep.tile([P, 3, BLOCKS, PLAIN, P], F32, name=f"weights{h}")
            for t in range(TURNED, PACK):
                for lists in (slice(0, 2), slice(2, 3)) if t == PACK - 1 else (slice(0, 3),):
                    nc.scalar.activation(
                        weights[:, lists, :, t - TURNED, :], products[:, t, lists, :].rearrange("p i (b j) -> p i b j", b=BLOCKS), ACT.Exp, bias=plus_shift[:], scale=quarter
                    )
            by_list = weights[:].rearrange("p i b t j -> p i (b t j)")
            pair = keep.tile([P, PLAIN * HALF], F32, name=f"pair{h}")
            nc.vector.tensor_tensor(pair[:], by_list[:, 0, :], by_list[:, 1, :], ALU.add)
            total = keep.tile([P, BLOCKS, PLAIN * P], F32, name=f"total{h}")
            nc.vector.tensor_tensor(total[:].rearrange("p b n -> p (b n)"), pair[:], by_list[:, 2, :], ALU.add)
            return sums, numerators, by_list, total

        def take_logs(h, sums, total):
            turned_bias, plain_bias = ln_biases()
            logs = keep.tile([P, BLOCKS, PACK * P], F32, name=f"logs{h}")
            for b in range(BLOCKS):
                nc.scalar.activation(logs[:, b, : TURNED * P], sums[b][:].rearrange("p t j -> p (t j)"), ACT.Ln, bias=turned_bias, scale=UNIT)
            nc.scalar.activation(logs[:, :, TURNED * P :], total[:], ACT.Ln, bias=plain_bias, scale=UNIT)
            return logs

        def invert(h, logs):
            inverses = []
            for b in range(BLOCKS):
                inverse = keep.tile([P, PACK * P], F32, name=f"inverse{h}{b}")
                nc.scalar.activation(inverse[:], logs[:, b, :], ACT.Exp, bias=minus_shift[:], scale=-1.0)
                inverses.append(inverse)
            return inverses

        out_rows = out_0.rearrange("(p t) j -> p t j", t=PACK)
        out_words = out_1[0].rearrange("p n r -> p (n r)").bitcast(I32)
        out_scales = keep.tile([P, S], U8, name="out_scales", align_bytes=64)

        def finish(h, inverses, numerators, by_list, weighted):
            nc.vector.scalar_tensor_tensor(weighted[:], by_list[:, 0, :], 2.0, by_list[:, 1, :], ALU.mult, ALU.add)
            for b in range(BLOCKS):
                columns = slice(h * HALF + b * P, h * HALF + (b + 1) * P)
                result = keep.tile([P, PACK * P], F32, name=f"result{h}{b}")
                nc.vector.scalar_tensor_tensor(
                    result[:, : TURNED * P], numerators[b][:].rearrange("p t j -> p (t j)"), 2.0, inverses[b][:, : TURNED * P], ALU.add, ALU.mult
                )
                nc.vector.tensor_tensor(result[:, TURNED * P :], weighted[:, b * PLAIN * P : (b + 1) * PLAIN * P], inverses[b][:, TURNED * P :], ALU.mult)
                nc.sync.dma_start(out_rows[:, :, columns], result[:].rearrange("p (t j) -> p t j", t=PACK))
                rounded = keep.tile([P, P, PACK], BF16, name=f"rounded{h}{b}", align_bytes=64)
                nc.vector.tensor_copy(rounded[:].rearrange("p (c i) t -> p c t i", i=4), result[:].rearrange("p (t c i) -> p c t i", t=PACK, i=4))
                codes = keep.tile([P, P], U32, name=f"out_codes{h}{b}", align_bytes=64)
                nc.vector.quantize_mx(out=codes[:].bitcast(FP8X4), scales=out_scales[:, columns], in_=rounded[:].rearrange("p j t -> p (j t)"))
                nc.sync.dma_start(out_words[:, columns], codes[:].bitcast(I32))

        products = keep.tile([P, PACK, 3, HALF], F32, name="products0")
        sums, first_numerators, first_by_list, total = exponentiate(0, products, look_up(0, products))
        first_logs = take_logs(0, sums, total)
        products = keep.tile([P, PACK, 3, HALF], F32, name="products1", tag="pair0")
        differences = look_up(1, products)
        first_inverses = invert(0, first_logs)
        sums, numerators, by_list, total = exponentiate(1, products, differences)
        finish(0, first_inverses, first_numerators, first_by_list, keep.tile([P, PLAIN * HALF], F32, name="weighted0", tag="pair1"))
        finish(1, invert(1, take_logs(1, sums, total)), numerators, by_list, keep.tile([P, PLAIN * HALF], F32, name="weighted1"))
        for q in range(QUADRANTS):
            queue = nc.scalar if q % 2 else nc.sync
            queue.dma_start(out_2[0][4 * q : 4 * q + 4, :].bitcast(I32), out_scales[32 * q : 32 * q + 4, :].bitcast(I32))
